import numpy as np
import ml_dtypes


def mxq(x, axis, fmt="e4m3"):
    dtype, down = {"e4m3": (ml_dtypes.float8_e4m3fn, 7), "e5m2": (ml_dtypes.float8_e5m2, 14)}[fmt]
    v = np.moveaxis(np.asarray(x, np.float32).astype(ml_dtypes.bfloat16).astype(np.float64), axis, -1)
    blocks = v.reshape(v.shape[:-1] + (-1, 32))
    amax = np.abs(blocks).max(-1, keepdims=True)
    byte = np.maximum(np.where(amax > 0, np.frexp(amax)[1] - 1 + 127, 0) - down, 1)
    scale = np.exp2(byte - 127.0)
    codes = (blocks / scale).astype(np.float32).astype(dtype).astype(np.float64)
    return np.moveaxis((codes * scale).reshape(v.shape), -1, axis)


WIDE = False


def mx_kscale(k):
    if not WIDE:
        return np.ones(k)
    levels = np.array([10, -10, 5, -5, 0])
    if k % 512:
        return np.exp2(np.random.permutation(np.resize(levels, k // 32))).repeat(32)
    a = np.empty((k // 512, 16))
    for p in range(k // 512):
        a[p, :8] = np.random.permutation(np.resize(levels, 8))
        for g in range(8):
            far = levels[np.abs(levels - a[p, g]) >= 10]
            a[p, g + 8] = far[np.random.randint(len(far))]
    return np.exp2(a.ravel()).repeat(32)


def f64(x):
    return np.asarray(x).astype(np.float64)


def striped(idx):
    return np.tile(idx.reshape(-1, 16).T, (8, 1)).astype(np.uint16)


def unstriped(offs):
    return offs[:16].T.reshape(-1).astype(np.int64)


def striped8(idx):
    return np.concatenate([x.reshape(-1, 16).T for x in idx]).astype(np.uint16)


def runs(offs, k):
    lists = np.stack([offs[16 * r : 16 * r + 16].T.reshape(-1) for r in range(8)]).astype(np.int64)
    return lists[np.arange(k) % 512 // 64]


def pack_weight(w):
    k, n = w.shape
    w = f64(np.asarray(w, np.float32).astype(ml_dtypes.bfloat16)).reshape(k // 32, 32, n)
    amax = np.abs(w).max(1)
    byte = np.clip(np.where(amax > 0, np.frexp(amax)[1] - 1 + 127 - 7, 1), 1, 254)
    scaled = (w * np.exp2(127.0 - byte)[:, None, :]).reshape(k, n).astype(np.float32)
    words = np.ascontiguousarray(scaled.reshape(k // 512, 128, 4, n).transpose(0, 1, 3, 2)).astype(ml_dtypes.float8_e4m3fn).view(np.uint8)
    return words, np.ascontiguousarray(byte.astype(np.uint8).reshape(k // 512, 16, n))


def unpack_weight(words, scales):
    g, p, n, _ = words.shape
    vals = np.ascontiguousarray(words).view(ml_dtypes.float8_e4m3fn).astype(np.float64) * np.repeat(np.exp2(scales.astype(np.float64) - 127.0), 8, axis=1)[..., None]
    return vals.transpose(0, 1, 3, 2).reshape(g * 512, n)


K, T, S, V, H, U = 512, 2048, 512, 512, 512, 1024


def setup_inputs():
    n = np.random.standard_normal
    s = mx_kscale(K)[:, None]
    u = mx_kscale(S)
    packed_xT = pack_weight(n((K, T)) * s)
    return {
        "x_words": packed_xT[0],
        "x_scales": packed_xT[1],
        "w1": (n((K, H)) / np.sqrt(K) / s).astype(np.float32),
        "w2": (n((K, H)) / np.sqrt(K) / s).astype(np.float32),
        "ga": (np.random.uniform(0.5, 1.5, (H, 1)) * u[:, None]).astype(np.float32),
        "gb": (np.random.uniform(0.5, 1.5, (H, 1)) / u[:, None]).astype(np.float32),
        "old": n((S, U)).astype(np.float32),
        "offs": striped(np.random.permutation(T)[:S]),
        "two": striped(np.random.permutation(T)[:V]),
        "n1": striped8(np.stack([np.random.permutation(S) for _ in range(8)])),
        "nq": striped8(np.stack([np.random.permutation(V) for _ in range(8)])),
        "slot": striped8(np.stack([np.random.permutation(U)[:V] for _ in range(8)])),
    }


def reference(x_words, x_scales, w1, w2, ga, gb, old, offs, two, n1, nq, slot):
    xq = unpack_weight(x_words, x_scales)[:, unstriped(offs)]
    a = mxq(f64(w1), 0, "e4m3").T @ xq
    z = f64(ga) * (a[np.arange(H)[:, None], runs(n1, H)])
    x_two = unpack_weight(x_words, x_scales)[:, unstriped(two)]
    b = mxq(f64(w2), 0, "e4m3").T @ x_two
    z2 = f64(gb) * (b - (b[np.arange(H)[:, None], runs(nq, H)]))
    s = 0.0625 * ((mxq(z, 0, "e4m3").T @ mxq(z2, 0, "e4m3")))
    nw = 0.5 * (s + f64(old)[np.arange(S)[:, None], runs(slot, S)])
    out = f64(old).copy()
    out[np.arange(S)[:, None], runs(slot, S)] = nw
    return out

@@ -1,0 +1,171 @@
+from contextlib import ExitStack
+
+import concourse.mybir as mybir
+
+K, T, S, V, H, U = 512, 2048, 512, 512, 512, 1024
+FLOPS = 3 * 2 * 512 * 512 * 512
+
+F32 = mybir.dt.float32
+BF16 = mybir.dt.bfloat16
+I32 = mybir.dt.int32
+U32 = mybir.dt.uint32
+U16 = mybir.dt.uint16
+U8 = mybir.dt.uint8
+FP8X4 = mybir.dt.float8_e4m3fn_x4
+COPY = mybir.ActivationFunctionType.Copy
+MULT = mybir.AluOpType.mult
+ADD = mybir.AluOpType.add
+SUB = mybir.AluOpType.subtract
+
+P = 128
+PACK = 4
+HALF = 256
+HCOL = HALF // 16
+
+
+def tile_picked_keyput_none_p_kernel(tc, x_words, x_scales, w1, w2, ga, gb, old, offs, two, n1, nq, slot, out):
+    nc = tc.nc
+    with ExitStack() as ctx:
+        keep = ctx.enter_context(tc.tile_pool(name="keep", bufs=1))
+        psum = ctx.enter_context(tc.psum_pool(name="psum", bufs=4))
+
+        def sb(name, shape, dtype, tag=None):
+            return keep.tile(shape, dtype, name=name, tag=tag or name, align_bytes=64)
+
+        lists = {}
+        for name in ("offs", "two", "n1", "nq", "slot"):
+            lists[name] = sb("list_" + name, [P, 32], U16)
+        xw = sb("xw", [P, T], U32)
+        xs = sb("xs", [P, T], U8)
+        w_raw = [sb("w_raw%d" % i, [P, PACK, H], F32) for i in range(2)]
+        gain = [sb("gain%d" % i, [P, PACK], F32) for i in range(2)]
+        page = [sb("page%d" % t, [P, U], F32) for t in range(PACK)]
+        old_rows = old.rearrange("(p t) u -> t p u", t=PACK)
+        out_rows = out.rearrange("(p t) u -> t p u", t=PACK)
+
+        nc.gpsimd.memset(xs[:].bitcast(I32), 0)
+        nc.sync.dma_start(lists["slot"][:], slot)
+        nc.sync.dma_start(page[0][:], old_rows[0])
+        for q in range(4):
+            nc.sync.dma_start(xs[32 * q : 32 * q + 4, :].bitcast(I32), x_scales[0, 4 * q : 4 * q + 4, :].bitcast(I32))
+        nc.sync.dma_start(lists["offs"][:], offs)
+        nc.sync.dma_start(w_raw[0][:], w1.rearrange("(p j) c -> p j c", j=PACK))
+        nc.sync.dma_start(lists["two"][:], two)
+        nc.sync.dma_start(page[1][:], old_rows[1])
+        nc.sync.dma_start(xw[:].bitcast(I32), x_words[0].rearrange("p n r -> p (n r)").bitcast(I32))
+        nc.sync.dma_start(gain[0][:], ga.rearrange("(p t) o -> p (t o)", t=PACK))
+        nc.sync.dma_start(lists["n1"][:], n1)
+        nc.sync.dma_start(w_raw[1][:], w2.rearrange("(p j) c -> p j c", j=PACK))
+        nc.sync.dma_start(gain[1][:], gb.rearrange("(p t) o -> p (t o)", t=PACK))
+        nc.sync.dma_start(lists["nq"][:], nq)
+        for t in range(2, PACK):
+            nc.sync.dma_start(page[t][:], old_rows[t])
+
+        def quantize(name, src, width):
+            codes = sb(name + "_codes", [P, width], U32)
+            scales = sb(name + "_scales", [P, width], U8)
+            nc.vector.quantize_mx(out=codes[:].bitcast(FP8X4), scales=scales[:], in_=src[:])
+            return codes, scales
+
+        def product(acc, stat, t, mov_codes, mov_scales):
+            cols = slice(P * t, P * (t + 1))
+            nc.tensor.matmul_mx(
+                out=acc[:], lhsT=stat[0][:, cols].bitcast(FP8X4), lhsT_scale=stat[1][:, cols],
+                rhs=mov_codes[:].bitcast(FP8X4), rhs_scale=mov_scales[:], start=True, stop=True,
+            )
+
+        def deal(dst, src, m0, m1):
+            nc.scalar.activation(
+                dst[:].rearrange("p (t m j) -> p m j t", t=PACK, j=PACK)[:, m0:m1],
+                src.rearrange("p j (m t) -> p m j t", t=PACK),
+                COPY,
+            )
+
+        half_old = {}
+
+        def fetch_old(t, tag=None):
+            half_old[t] = sb("half_old%d" % t, [P, V], F32, tag)
+            nc.vector.tensor_scalar(half_old[t][:], page[t][:].indirect(lists["slot"][:]), 0.5, 0.0, MULT, ADD)
+
+        tok_w = [sb("tok_w%d" % i, [P, S], U32) for i in range(2)]
+        tok_s = [sb("tok_s%d" % i, [P, S], U8) for i in range(2)]
+        fetch_old(0)
+        for i, name in enumerate(("offs", "two")):
+            nc.vector.tensor_copy(tok_s[i][:], xs[:].indirect(lists[name][:]))
+        fetch_old(1)
+        w_bf = [sb("w_bf%d" % i, [P, PACK * H], BF16) for i in range(2)]
+        deal(w_bf[0], w_raw[0][:], 0, P)
+        w1q = quantize("w1", w_bf[0], H)
+        for i, name in enumerate(("offs", "two")):
+            nc.vector.tensor_copy(tok_w[i][:], xw[:].indirect(lists[name][:]))
+        a_sb = [sb("a%d" % t, [P, S], F32) for t in range(PACK)]
+        for t in range(PACK):
+            acc = psum.tile([P, S], F32, name="acc_a", tag="first")
+            product(acc, w1q, t, tok_w[0], tok_s[0])
+            nc.scalar.activation(a_sb[t][:], acc[:], COPY, scale=gain[0][:, t : t + 1])
+        deal(w_bf[1], w_raw[1][:], 0, P)
+
+        z32 = [sb("z32_%d" % h, [P, PACK, HALF], F32) for h in range(2)]
+        for h in range(2):
+            for t in range(PACK):
+                nc.vector.tensor_copy(z32[h][:, t, :], a_sb[t][:].indirect(lists["n1"][:, HCOL * h : HCOL * (h + 1)]))
+        w2q = quantize("w2", w_bf[1], H)
+        fetch_old(2, "w_raw1")
+        z_bf = sb("z_bf", [P, PACK * S], BF16)
+        deal(z_bf, z32[0][:], 0, 64)
+        b_win = [sb("b_win%d" % t, [P, V], F32) for t in range(PACK)]
+        b_own = [[sb("b_own%d_%d" % (h, t), [P, HALF], F32) for t in range(PACK)] for h in range(2)]
+        acc_b = []
+        for t in range(PACK):
+            acc = psum.tile([P, V], F32, name="acc_b", tag="second")
+            acc_b.append(acc)
+            product(acc, w2q, t, tok_w[1], tok_s[1])
+            nc.scalar.activation(b_win[t][:], acc[:], COPY, scale=gain[1][:, t : t + 1])
+            nc.scalar.activation(b_own[0][t][:], acc[:, :HALF], COPY, scale=gain[1][:, t : t + 1])
+        for t in range(PACK):
+            nc.scalar.activation(b_own[1][t][:], acc_b[t][:, HALF:], COPY, scale=gain[1][:, t : t + 1])
+        deal(z_bf, z32[1][:], 64, 128)
+
+        d32 = [sb("d32_%d" % h, [P, PACK, HALF], F32) for h in range(2)]
+        z2_bf = [sb("z2_bf%d" % h, [P, PACK * HALF], BF16) for h in range(2)]
+        for h in range(2):
+            for t in range(PACK):
+                nc.vector.tensor_tensor(
+                    d32[h][:, t, :], b_win[t][:].indirect(lists["nq"][:, HCOL * h : HCOL * (h + 1)]),
+                    b_own[h][t][:], SUB,
+                )
+            nc.scalar.activation(
+                z2_bf[h][:].rearrange("p (c i j) -> p c j i", i=4, j=PACK),
+                d32[h][:].rearrange("p j (c i) -> p c j i", i=4),
+                COPY, scale=-1.0,
+            )
+        zq = quantize("z", z_bf, S)
+        z2q = [quantize("z2_0", z2_bf[0], HALF)]
+        fetch_old(3, "d32_0")
+        z2q.append(quantize("z2_1", z2_bf[1], HALF))
+        s_sb = [sb("s%d" % t, [P, V], F32) for t in range(PACK)]
+
+        def score(t, h):
+            acc = psum.tile([P, HALF], F32, name="acc_s", tag=("first", "second")[h])
+            product(acc, zq, t, z2q[h][0], z2q[h][1])
+            nc.scalar.activation(s_sb[t][:, HALF * h : HALF * (h + 1)], acc[:], COPY, scale=0.03125)
+
+        def put(t, c0, c1):
+            nc.vector.tensor_tensor(
+                page[t][:].indirect(lists["slot"][:, c0 // 16 : c1 // 16]), s_sb[t][:, c0:c1], half_old[t][:, c0:c1], ADD,
+            )
+
+        score(0, 0)
+        put(0, 0, HALF)
+        score(1, 0)
+        score(1, 1)
+        put(1, 0, V)
+        nc.sync.dma_start(out_rows[1], page[1][:])
+        score(0, 1)
+        put(0, HALF, V)
+        nc.sync.dma_start(out_rows[0], page[0][:])
+        for t in range(2, PACK):
+            score(t, 0)
+            score(t, 1)
+            put(t, 0, V)
+            nc.sync.dma_start(out_rows[t], page[t][:])

@@ -27,6 +27,7 @@ def tile_picked_keyput_none_p_kernel(tc, x_words, x_scales, w1, w2, ga, gb, old,
     nc = tc.nc
     with ExitStack() as ctx:
         keep = ctx.enter_context(tc.tile_pool(name="keep", bufs=1))
+        reuse = ctx.enter_context(tc.tile_pool(name="reuse", bufs=1))
         psum = ctx.enter_context(tc.psum_pool(name="psum", bufs=4))
 
         def sb(name, shape, dtype, tag=None):
@@ -37,29 +38,32 @@ def tile_picked_keyput_none_p_kernel(tc, x_words, x_scales, w1, w2, ga, gb, old,
             lists[name] = sb("list_" + name, [P, 32], U16)
         xw = sb("xw", [P, T], U32)
         xs = sb("xs", [P, T], U8)
-        w_raw = [sb("w_raw%d" % i, [P, PACK, H], F32) for i in range(2)]
+        w1_raw = sb("w1_raw", [P, PACK, H], F32)
+        w2_raw = [sb("w2_raw0", [P, PACK, HALF], F32), reuse.tile([P, 3 * PACK, HALF], F32, name="w2_raw1", offset=8 * S)]
         gain = [sb("gain%d" % i, [P, PACK], F32) for i in range(2)]
         page = [sb("page%d" % t, [P, U], F32) for t in range(PACK)]
         old_rows = old.rearrange("(p t) u -> t p u", t=PACK)
         out_rows = out.rearrange("(p t) u -> t p u", t=PACK)
 
         nc.gpsimd.memset(xs[:].bitcast(I32), 0)
+        w2_rows = w2.rearrange("(p j) c -> p j c", j=PACK)
         nc.sync.dma_start(lists["slot"][:], slot)
         nc.sync.dma_start(page[0][:], old_rows[0])
         for q in range(4):
             nc.sync.dma_start(xs[32 * q : 32 * q + 4, :].bitcast(I32), x_scales[0, 4 * q : 4 * q + 4, :].bitcast(I32))
         nc.sync.dma_start(lists["offs"][:], offs)
-        nc.sync.dma_start(w_raw[0][:], w1.rearrange("(p j) c -> p j c", j=PACK))
+        nc.sync.dma_start(w1_raw[:], w1.rearrange("(p j) c -> p j c", j=PACK))
         nc.sync.dma_start(lists["two"][:], two)
         nc.sync.dma_start(page[1][:], old_rows[1])
         nc.sync.dma_start(xw[:].bitcast(I32), x_words[0].rearrange("p n r -> p (n r)").bitcast(I32))
+        nc.sync.dma_start(w2_raw[0][:], w2_rows[:, :, :HALF])
         nc.sync.dma_start(gain[0][:], ga.rearrange("(p t) o -> p (t o)", t=PACK))
+        nc.sync.dma_start(page[2][:], old_rows[2])
         nc.sync.dma_start(lists["n1"][:], n1)
-        nc.sync.dma_start(w_raw[1][:], w2.rearrange("(p j) c -> p j c", j=PACK))
+        nc.sync.dma_start(w2_raw[1][:, :PACK], w2_rows[:, :, HALF:])
         nc.sync.dma_start(gain[1][:], gb.rearrange("(p t) o -> p (t o)", t=PACK))
         nc.sync.dma_start(lists["nq"][:], nq)
-        for t in range(2, PACK):
-            nc.sync.dma_start(page[t][:], old_rows[t])
+        nc.sync.dma_start(page[3][:], old_rows[3])
 
         def quantize(name, src, width):
             codes = sb(name + "_codes", [P, width], U32)
@@ -83,48 +87,43 @@ def tile_picked_keyput_none_p_kernel(tc, x_words, x_scales, w1, w2, ga, gb, old,
 
         half_old = {}
 
-        def fetch_old(t, tag=None):
-            half_old[t] = sb("half_old%d" % t, [P, V], F32, tag)
-            nc.vector.tensor_scalar(half_old[t][:], page[t][:].indirect(lists["slot"][:]), 0.5, 0.0, MULT, ADD)
+        def fetch_old(t, dst):
+            half_old[t] = dst
+            nc.vector.tensor_scalar(dst, page[t][:].indirect(lists["slot"][:]), 0.5, 0.0, MULT, ADD)
 
-        tok_w = [sb("tok_w%d" % i, [P, S], U32) for i in range(2)]
         tok_s = [sb("tok_s%d" % i, [P, S], U8) for i in range(2)]
-        fetch_old(0)
+        fetch_old(0, sb("half_old0", [P, V], F32)[:])
         for i, name in enumerate(("offs", "two")):
             nc.vector.tensor_copy(tok_s[i][:], xs[:].indirect(lists[name][:]))
-        fetch_old(1)
+        fetch_old(1, sb("half_old1", [P, V], F32)[:])
         w_bf = [sb("w_bf%d" % i, [P, PACK * H], BF16) for i in range(2)]
-        deal(w_bf[0], w_raw[0][:], 0, P)
+        deal(w_bf[0], w1_raw[:], 0, P)
         w1q = quantize("w1", w_bf[0], H)
+        tok_w = [sb("tok_w%d" % i, [P, S], U32) for i in range(2)]
         for i, name in enumerate(("offs", "two")):
             nc.vector.tensor_copy(tok_w[i][:], xw[:].indirect(lists[name][:]))
-        a_sb = [sb("a%d" % t, [P, S], F32) for t in range(PACK)]
+        fetch_old(2, sb("half_old2", [P, V], F32)[:])
+        deal(w_bf[1], w2_raw[0][:], 0, 64)
+        a_sb = {}
+        z32 = sb("z32", [P, PACK, S], F32)
         for t in range(PACK):
             acc = psum.tile([P, S], F32, name="acc_a", tag="first")
             product(acc, w1q, t, tok_w[0], tok_s[0])
-            nc.scalar.activation(a_sb[t][:], acc[:], COPY, scale=gain[0][:, t : t + 1])
-        deal(w_bf[1], w_raw[1][:], 0, P)
+            a_sb[t] = reuse.tile([P, 2 * S], F32, name="a%d" % t, offset=8 * S * t)
+            nc.scalar.activation(a_sb[t][:, :S], acc[:], COPY, scale=gain[0][:, t : t + 1])
+            nc.vector.tensor_copy(z32[:, t, :], a_sb[t][:].indirect(lists["n1"][:]))
+            if t == 0:
+                deal(w_bf[1], w2_raw[1][:, :PACK], 64, 128)
+                w2q = quantize("w2", w_bf[1], H)
 
-        z32 = [sb("z32_%d" % h, [P, PACK, HALF], F32) for h in range(2)]
-        for h in range(2):
-            for t in range(PACK):
-                nc.vector.tensor_copy(z32[h][:, t, :], a_sb[t][:].indirect(lists["n1"][:, HCOL * h : HCOL * (h + 1)]))
-        w2q = quantize("w2", w_bf[1], H)
-        fetch_old(2, "w_raw1")
-        z_bf = sb("z_bf", [P, PACK * S], BF16)
-        deal(z_bf, z32[0][:], 0, 64)
         b_win = [sb("b_win%d" % t, [P, V], F32) for t in range(PACK)]
         b_own = [[sb("b_own%d_%d" % (h, t), [P, HALF], F32) for t in range(PACK)] for h in range(2)]
-        acc_b = []
         for t in range(PACK):
             acc = psum.tile([P, V], F32, name="acc_b", tag="second")
-            acc_b.append(acc)
             product(acc, w2q, t, tok_w[1], tok_s[1])
             nc.scalar.activation(b_win[t][:], acc[:], COPY, scale=gain[1][:, t : t + 1])
             nc.scalar.activation(b_own[0][t][:], acc[:, :HALF], COPY, scale=gain[1][:, t : t + 1])
-        for t in range(PACK):
-            nc.scalar.activation(b_own[1][t][:], acc_b[t][:, HALF:], COPY, scale=gain[1][:, t : t + 1])
-        deal(z_bf, z32[1][:], 64, 128)
+            nc.sync.dma_start(b_own[1][t][:], b_win[t][:, HALF:])
 
         d32 = [sb("d32_%d" % h, [P, PACK, HALF], F32) for h in range(2)]
         z2_bf = [sb("z2_bf%d" % h, [P, PACK * HALF], BF16) for h in range(2)]
@@ -134,6 +133,9 @@ def tile_picked_keyput_none_p_kernel(tc, x_words, x_scales, w1, w2, ga, gb, old,
                     d32[h][:, t, :], b_win[t][:].indirect(lists["nq"][:, HCOL * h : HCOL * (h + 1)]),
                     b_own[h][t][:], SUB,
                 )
+            if h == 0:
+                z_bf = sb("z_bf", [P, PACK * S], BF16, "b_own0_0")
+                deal(z_bf, z32[:], 0, P)
             nc.scalar.activation(
                 z2_bf[h][:].rearrange("p (c i j) -> p c j i", i=4, j=PACK),
                 d32[h][:].rearrange("p j (c i) -> p c j i", i=4),
@@ -141,7 +143,7 @@ def tile_picked_keyput_none_p_kernel(tc, x_words, x_scales, w1, w2, ga, gb, old,
             )
         zq = quantize("z", z_bf, S)
         z2q = [quantize("z2_0", z2_bf[0], HALF)]
-        fetch_old(3, "d32_0")
+        fetch_old(3, sb("half_old3", [P, V], F32, "d32_0")[:])
         z2q.append(quantize("z2_1", z2_bf[1], HALF))
         s_sb = [sb("s%d" % t, [P, V], F32) for t in range(PACK)]
 

@@ -54,16 +54,16 @@ def tile_picked_keyput_none_p_kernel(tc, x_words, x_scales, w1, w2, ga, gb, old,
         nc.sync.dma_start(lists["offs"][:], offs)
         nc.sync.dma_start(w1_raw[:], w1.rearrange("(p j) c -> p j c", j=PACK))
         nc.sync.dma_start(lists["two"][:], two)
-        nc.sync.dma_start(page[1][:], old_rows[1])
         nc.sync.dma_start(xw[:].bitcast(I32), x_words[0].rearrange("p n r -> p (n r)").bitcast(I32))
         nc.sync.dma_start(w2_raw[0][:], w2_rows[:, :, :HALF])
         nc.sync.dma_start(gain[0][:], ga.rearrange("(p t) o -> p (t o)", t=PACK))
-        nc.sync.dma_start(page[2][:], old_rows[2])
+        nc.sync.dma_start(page[1][:], old_rows[1])
         nc.sync.dma_start(lists["n1"][:], n1)
         nc.sync.dma_start(w2_raw[1][:, :PACK], w2_rows[:, :, HALF:])
         nc.sync.dma_start(gain[1][:], gb.rearrange("(p t) o -> p (t o)", t=PACK))
         nc.sync.dma_start(lists["nq"][:], nq)
-        nc.sync.dma_start(page[3][:], old_rows[3])
+        for t in range(2, PACK):
+            nc.sync.dma_start(page[t][:], old_rows[t])
 
         def quantize(name, src, width):
             codes = sb(name + "_codes", [P, width], U32)
@@ -95,14 +95,14 @@ def tile_picked_keyput_none_p_kernel(tc, x_words, x_scales, w1, w2, ga, gb, old,
         fetch_old(0, sb("half_old0", [P, V], F32)[:])
         for i, name in enumerate(("offs", "two")):
             nc.vector.tensor_copy(tok_s[i][:], xs[:].indirect(lists[name][:]))
-        fetch_old(1, sb("half_old1", [P, V], F32)[:])
         w_bf = [sb("w_bf%d" % i, [P, PACK * H], BF16) for i in range(2)]
         deal(w_bf[0], w1_raw[:], 0, P)
+        tok_w = [sb("tok_w0", [P, S], U32)]
+        nc.vector.tensor_copy(tok_w[0][:], xw[:].indirect(lists["offs"][:]))
         w1q = quantize("w1", w_bf[0], H)
-        tok_w = [sb("tok_w%d" % i, [P, S], U32) for i in range(2)]
-        for i, name in enumerate(("offs", "two")):
-            nc.vector.tensor_copy(tok_w[i][:], xw[:].indirect(lists[name][:]))
-        fetch_old(2, sb("half_old2", [P, V], F32)[:])
+        tok_w.append(sb("tok_w1", [P, S], U32, "w1_raw"))
+        nc.vector.tensor_copy(tok_w[1][:], xw[:].indirect(lists["two"][:]))
+        fetch_old(1, sb("half_old1", [P, V], F32)[:])
         deal(w_bf[1], w2_raw[0][:], 0, 64)
         a_sb = {}
         z32 = sb("z32", [P, PACK, S], F32)
@@ -118,12 +118,15 @@ def tile_picked_keyput_none_p_kernel(tc, x_words, x_scales, w1, w2, ga, gb, old,
 
         b_win = [sb("b_win%d" % t, [P, V], F32) for t in range(PACK)]
         b_own = [[sb("b_own%d_%d" % (h, t), [P, HALF], F32) for t in range(PACK)] for h in range(2)]
+        acc_b = []
         for t in range(PACK):
             acc = psum.tile([P, V], F32, name="acc_b", tag="second")
+            acc_b.append(acc)
             product(acc, w2q, t, tok_w[1], tok_s[1])
             nc.scalar.activation(b_win[t][:], acc[:], COPY, scale=gain[1][:, t : t + 1])
             nc.scalar.activation(b_own[0][t][:], acc[:, :HALF], COPY, scale=gain[1][:, t : t + 1])
-            nc.sync.dma_start(b_own[1][t][:], b_win[t][:, HALF:])
+        for t in range(PACK):
+            nc.scalar.activation(b_own[1][t][:], acc_b[t][:, HALF:], COPY, scale=gain[1][:, t : t + 1])
 
         d32 = [sb("d32_%d" % h, [P, PACK, HALF], F32) for h in range(2)]
         z2_bf = [sb("z2_bf%d" % h, [P, PACK * HALF], BF16) for h in range(2)]
@@ -141,6 +144,7 @@ def tile_picked_keyput_none_p_kernel(tc, x_words, x_scales, w1, w2, ga, gb, old,
                 d32[h][:].rearrange("p j (c i) -> p c j i", i=4),
                 COPY, scale=-1.0,
             )
+        fetch_old(2, sb("half_old2", [P, V], F32, "b_own1_2")[:])
         zq = quantize("z", z_bf, S)
         z2q = [quantize("z2_0", z2_bf[0], HALF)]
         fetch_old(3, sb("half_old3", [P, V], F32, "d32_0")[:])

from contextlib import ExitStack

import concourse.mybir as mybir

K, T, S, V, H, U = 512, 2048, 512, 512, 512, 1024
FLOPS = 3 * 2 * 512 * 512 * 512

F32 = mybir.dt.float32
BF16 = mybir.dt.bfloat16
I32 = mybir.dt.int32
U32 = mybir.dt.uint32
U16 = mybir.dt.uint16
U8 = mybir.dt.uint8
FP8X4 = mybir.dt.float8_e4m3fn_x4
COPY = mybir.ActivationFunctionType.Copy
MULT = mybir.AluOpType.mult
ADD = mybir.AluOpType.add
SUB = mybir.AluOpType.subtract

P = 128
PACK = 4
HALF = 256
HCOL = HALF // 16


def tile_picked_keyput_none_p_kernel(tc, x_words, x_scales, w1, w2, ga, gb, old, offs, two, n1, nq, slot, out):
    nc = tc.nc
    with ExitStack() as ctx:
        keep = ctx.enter_context(tc.tile_pool(name="keep", bufs=1))
        reuse = ctx.enter_context(tc.tile_pool(name="reuse", bufs=1))
        psum = ctx.enter_context(tc.psum_pool(name="psum", bufs=4))

        def sb(name, shape, dtype, tag=None):
            return keep.tile(shape, dtype, name=name, tag=tag or name, align_bytes=64)

        lists = {}
        for name in ("offs", "two", "n1", "nq", "slot"):
            lists[name] = sb("list_" + name, [P, 32], U16)
        xw = sb("xw", [P, T], U32)
        xs = sb("xs", [P, T], U8)
        w1_raw = sb("w1_raw", [P, PACK, H], F32)
        w2_raw = [sb("w2_raw0", [P, PACK, HALF], F32), reuse.tile([P, 3 * PACK, HALF], F32, name="w2_raw1", offset=8 * S)]
        gain = [sb("gain%d" % i, [P, PACK], F32) for i in range(2)]
        page = [sb("page%d" % t, [P, U], F32) for t in range(PACK)]
        old_rows = old.rearrange("(p t) u -> t p u", t=PACK)
        out_rows = out.rearrange("(p t) u -> t p u", t=PACK)

        nc.gpsimd.memset(xs[:].bitcast(I32), 0)
        w2_rows = w2.rearrange("(p j) c -> p j c", j=PACK)
        nc.sync.dma_start(lists["slot"][:], slot)
        nc.sync.dma_start(page[0][:], old_rows[0])
        for q in range(4):
            nc.sync.dma_start(xs[32 * q : 32 * q + 4, :].bitcast(I32), x_scales[0, 4 * q : 4 * q + 4, :].bitcast(I32))
        nc.sync.dma_start(lists["offs"][:], offs)
        nc.sync.dma_start(w1_raw[:], w1.rearrange("(p j) c -> p j c", j=PACK))
        nc.sync.dma_start(lists["two"][:], two)
        nc.sync.dma_start(xw[:].bitcast(I32), x_words[0].rearrange("p n r -> p (n r)").bitcast(I32))
        nc.sync.dma_start(w2_raw[0][:], w2_rows[:, :, :HALF])
        nc.sync.dma_start(gain[0][:], ga.rearrange("(p t) o -> p (t o)", t=PACK))
        nc.sync.dma_start(page[1][:], old_rows[1])
        nc.sync.dma_start(lists["n1"][:], n1)
        nc.sync.dma_start(w2_raw[1][:, :PACK], w2_rows[:, :, HALF:])
        nc.sync.dma_start(gain[1][:], gb.rearrange("(p t) o -> p (t o)", t=PACK))
        nc.sync.dma_start(lists["nq"][:], nq)
        for t in range(2, PACK):
            nc.sync.dma_start(page[t][:], old_rows[t])

        def quantize(name, src, width):
            codes = sb(name + "_codes", [P, width], U32)
            scales = sb(name + "_scales", [P, width], U8)
            nc.vector.quantize_mx(out=codes[:].bitcast(FP8X4), scales=scales[:], in_=src[:])
            return codes, scales

        def product(acc, stat, t, mov_codes, mov_scales):
            cols = slice(P * t, P * (t + 1))
            nc.tensor.matmul_mx(
                out=acc[:], lhsT=stat[0][:, cols].bitcast(FP8X4), lhsT_scale=stat[1][:, cols],
                rhs=mov_codes[:].bitcast(FP8X4), rhs_scale=mov_scales[:], start=True, stop=True,
            )

        def deal(dst, src, m0, m1):
            nc.scalar.activation(
                dst[:].rearrange("p (t m j) -> p m j t", t=PACK, j=PACK)[:, m0:m1],
                src.rearrange("p j (m t) -> p m j t", t=PACK),
                COPY,
            )

        half_old = {}

        def fetch_old(t, dst):
            half_old[t] = dst
            nc.vector.tensor_scalar(dst, page[t][:].indirect(lists["slot"][:]), 0.5, 0.0, MULT, ADD)

        tok_s = [sb("tok_s%d" % i, [P, S], U8) for i in range(2)]
        fetch_old(0, sb("half_old0", [P, V], F32)[:])
        for i, name in enumerate(("offs", "two")):
            nc.vector.tensor_copy(tok_s[i][:], xs[:].indirect(lists[name][:]))
        w_bf = [sb("w_bf%d" % i, [P, PACK * H], BF16) for i in range(2)]
        deal(w_bf[0], w1_raw[:], 0, P)
        tok_w = [sb("tok_w0", [P, S], U32)]
        nc.vector.tensor_copy(tok_w[0][:], xw[:].indirect(lists["offs"][:]))
        w1q = quantize("w1", w_bf[0], H)
        tok_w.append(sb("tok_w1", [P, S], U32, "w1_raw"))
        nc.vector.tensor_copy(tok_w[1][:], xw[:].indirect(lists["two"][:]))
        fetch_old(1, sb("half_old1", [P, V], F32)[:])
        deal(w_bf[1], w2_raw[0][:], 0, 64)
        a_sb = {}
        z32 = sb("z32", [P, PACK, S], F32)
        for t in range(PACK):
            acc = psum.tile([P, S], F32, name="acc_a", tag="first")
            product(acc, w1q, t, tok_w[0], tok_s[0])
            a_sb[t] = reuse.tile([P, 2 * S], F32, name="a%d" % t, offset=8 * S * t)
            nc.scalar.activation(a_sb[t][:, :S], acc[:], COPY, scale=gain[0][:, t : t + 1])
            nc.vector.tensor_copy(z32[:, t, :], a_sb[t][:].indirect(lists["n1"][:]))
            if t == 0:
                deal(w_bf[1], w2_raw[1][:, :PACK], 64, 128)
                w2q = quantize("w2", w_bf[1], H)

        b_win = [sb("b_win%d" % t, [P, V], F32) for t in range(PACK)]
        b_own = [[sb("b_own%d_%d" % (h, t), [P, HALF], F32) for t in range(PACK)] for h in range(2)]
        acc_b = []
        for t in range(PACK):
            acc = psum.tile([P, V], F32, name="acc_b", tag="second")
            acc_b.append(acc)
            product(acc, w2q, t, tok_w[1], tok_s[1])
            nc.scalar.activation(b_win[t][:], acc[:], COPY, scale=gain[1][:, t : t + 1])
            nc.scalar.activation(b_own[0][t][:], acc[:, :HALF], COPY, scale=gain[1][:, t : t + 1])
        for t in range(PACK):
            nc.scalar.activation(b_own[1][t][:], acc_b[t][:, HALF:], COPY, scale=gain[1][:, t : t + 1])

        d32 = [sb("d32_%d" % h, [P, PACK, HALF], F32) for h in range(2)]
        z2_bf = [sb("z2_bf%d" % h, [P, PACK * HALF], BF16) for h in range(2)]
        for h in range(2):
            for t in range(PACK):
                nc.vector.tensor_tensor(
                    d32[h][:, t, :], b_win[t][:].indirect(lists["nq"][:, HCOL * h : HCOL * (h + 1)]),
                    b_own[h][t][:], SUB,
                )
            if h == 0:
                z_bf = sb("z_bf", [P, PACK * S], BF16, "b_own0_0")
                deal(z_bf, z32[:], 0, P)
            nc.scalar.activation(
                z2_bf[h][:].rearrange("p (c i j) -> p c j i", i=4, j=PACK),
                d32[h][:].rearrange("p j (c i) -> p c j i", i=4),
                COPY, scale=-1.0,
            )
        fetch_old(2, sb("half_old2", [P, V], F32, "b_own1_2")[:])
        zq = quantize("z", z_bf, S)
        z2q = [quantize("z2_0", z2_bf[0], HALF)]
        fetch_old(3, sb("half_old3", [P, V], F32, "d32_0")[:])
        z2q.append(quantize("z2_1", z2_bf[1], HALF))
        s_sb = [sb("s%d" % t, [P, V], F32) for t in range(PACK)]

        def score(t, h):
            acc = psum.tile([P, HALF], F32, name="acc_s", tag=("first", "second")[h])
            product(acc, zq, t, z2q[h][0], z2q[h][1])
            nc.scalar.activation(s_sb[t][:, HALF * h : HALF * (h + 1)], acc[:], COPY, scale=0.03125)

        def put(t, c0, c1):
            nc.vector.tensor_tensor(
                page[t][:].indirect(lists["slot"][:, c0 // 16 : c1 // 16]), s_sb[t][:, c0:c1], half_old[t][:, c0:c1], ADD,
            )

        score(0, 0)
        put(0, 0, HALF)
        score(1, 0)
        score(1, 1)
        put(1, 0, V)
        nc.sync.dma_start(out_rows[1], page[1][:])
        score(0, 1)
        put(0, HALF, V)
        nc.sync.dma_start(out_rows[0], page[0][:])
        for t in range(2, PACK):
            score(t, 0)
            score(t, 1)
            put(t, 0, V)
            nc.sync.dma_start(out_rows[t], page[t][:])
